import numpy as np
import ml_dtypes


def mxq(x, axis, fmt="e4m3"):
    dtype, down = {"e4m3": (ml_dtypes.float8_e4m3fn, 7), "e5m2": (ml_dtypes.float8_e5m2, 14)}[fmt]
    v = np.moveaxis(np.asarray(x, np.float32).astype(ml_dtypes.bfloat16).astype(np.float64), axis, -1)
    blocks = v.reshape(v.shape[:-1] + (-1, 32))
    amax = np.abs(blocks).max(-1, keepdims=True)
    byte = np.maximum(np.where(amax > 0, np.frexp(amax)[1] - 1 + 127, 0) - down, 1)
    scale = np.exp2(byte - 127.0)
    codes = (blocks / scale).astype(np.float32).astype(dtype).astype(np.float64)
    return np.moveaxis((codes * scale).reshape(v.shape), -1, axis)


WIDE = False


def mx_kscale(k):
    if not WIDE:
        return np.ones(k)
    levels = np.array([10, -10, 5, -5, 0])
    if k % 512:
        return np.exp2(np.random.permutation(np.resize(levels, k // 32))).repeat(32)
    a = np.empty((k // 512, 16))
    for p in range(k // 512):
        a[p, :8] = np.random.permutation(np.resize(levels, 8))
        for g in range(8):
            far = levels[np.abs(levels - a[p, g]) >= 10]
            a[p, g + 8] = far[np.random.randint(len(far))]
    return np.exp2(a.ravel()).repeat(32)


def f64(x):
    return np.asarray(x).astype(np.float64)


def striped(idx):
    return np.tile(np.asarray(idx).reshape(-1, 16).T, (8, 1)).astype(np.uint16)


def unstriped(offs):
    return offs[:16].T.reshape(-1).astype(np.int64)


E2M1 = np.array([0.0, 0.5, 1.0, 1.5, 2.0, 3.0, 4.0, 6.0, -0.0, -0.5, -1.0, -1.5, -2.0, -3.0, -4.0, -6.0])


def pack_weight(w, fmt):
    k, n = w.shape
    w = f64(np.asarray(w, np.float32).astype(ml_dtypes.bfloat16)).reshape(k // 32, 32, n)
    amax = np.abs(w).max(1)
    if fmt == "e4m3":
        byte = np.frexp(amax)[1] - 1 + 127 - 7
    else:
        mant, ex = np.frexp(amax / 6.0)
        byte = np.where(mant > 0.5, ex, ex - 1) + 127
    byte = np.clip(np.where(amax > 0, byte, 1), 1, 254)
    scaled = (w * np.exp2(127.0 - byte)[:, None, :]).reshape(k, n).astype(np.float32)
    by_word = np.ascontiguousarray(scaled.reshape(k // 512, 128, 4, n).transpose(0, 1, 3, 2))
    if fmt == "e4m3":
        words = by_word.astype(ml_dtypes.float8_e4m3fn).view(np.uint8)
    else:
        c = by_word.astype(ml_dtypes.float4_e2m1fn).view(np.uint8) & 0xF
        words = (c[..., 0::2] | (c[..., 1::2] << 4)).reshape(k // 512, 128, 2 * n)
    return np.ascontiguousarray(words), np.ascontiguousarray(byte.astype(np.uint8).reshape(k // 512, 16, n))


def unpack_weight(words, scales, fmt):
    g, _, n = scales.shape
    words = np.ascontiguousarray(words).reshape(g, 128, n, -1)
    if fmt == "e4m3":
        vals = words.view(ml_dtypes.float8_e4m3fn).astype(np.float64)
    else:
        nib = np.empty((g, 128, n, 4), np.uint8)
        nib[..., 0::2] = words & 0xF
        nib[..., 1::2] = words >> 4
        vals = E2M1[nib]
    vals = vals * np.repeat(np.exp2(scales.astype(np.float64) - 127.0), 8, axis=1)[..., None]
    return vals.transpose(0, 1, 3, 2).reshape(g * 512, n)


B, N, T, D, DV, NQ = 1, 1024, 4096, 512, 128, 128
PAGE = 512


def setup_inputs():
    n = np.random.standard_normal
    pages = np.random.permutation(T // PAGE)[:B * N // PAGE]
    idx = (pages[:, None] * PAGE + np.arange(PAGE)[None, :]).reshape(-1)
    s = mx_kscale(D)[:, None]
    u = np.ones(T)
    u[idx] = mx_kscale(B * N)
    r = np.random.uniform(0.5, 2.0, T)
    qp = [pack_weight(x, "e4m3") for x in n((B, D, NQ)) * s * (0.80 / np.sqrt(D))]
    k = n((D, T)) / s
    v = n((DV, T)) / (u * r)
    kp = pack_weight(k, "e4m3")
    vp = pack_weight(v.T, "e4m3")
    return {
        "q_words": np.stack([x[0] for x in qp]),
        "q_scales": np.stack([x[1] for x in qp]),
        "k_words": kp[0],
        "k_scales": kp[1],
        "v_words": vp[0],
        "v_scales": vp[1],
        "vs": np.tile(u * r, (128, 1)).astype(np.float32),
        "kb": np.tile(n(T), (128, 1)).astype(np.float32),
        "og": n((B, NQ, DV)).astype(np.float32),
        "offs": striped(idx),
        "voffs": striped((pages[:, None] * DV + np.arange(DV)[None, :]).reshape(-1)),
    }


def reference(q_words, q_scales, k_words, k_scales, v_words, v_scales, vs, kb, og, offs, voffs):
    idx = unstriped(offs)
    k = unpack_weight(k_words, k_scales, "e4m3")
    v = unpack_weight(v_words, v_scales, "e4m3")
    v = v.reshape(T // 512, 512, DV)[unstriped(voffs)[::DV] // DV].reshape(B, N, DV)
    pick = lambda x: x[:, idx].reshape(x.shape[0], B, N).transpose(1, 0, 2)
    q = np.stack([unpack_weight(q_words[b], q_scales[b], "e4m3") for b in range(B)])
    score = q.transpose(0, 2, 1) @ pick(k)
    score = score + pick(f64(kb))[:, :1, :]
    p = np.square(np.maximum(score, 0.0))
    total = p.sum(-1, keepdims=True) + 1.0
    w = p * pick(f64(vs))[:, :1, :]
    y = mxq(w, 2, "e4m3") @ v
    y = y / total
    y = y / (1.0 + np.exp(-f64(og)))
    return y

@@ -1,0 +1,177 @@
+from contextlib import ExitStack
+
+import concourse.mybir as mybir
+from concourse.masks import make_identity
+
+F32 = mybir.dt.float32
+BF16 = mybir.dt.bfloat16
+I32 = mybir.dt.int32
+U32 = mybir.dt.uint32
+U16 = mybir.dt.uint16
+U8 = mybir.dt.uint8
+FP8X4 = mybir.dt.float8_e4m3fn_x4
+ACT = mybir.ActivationFunctionType
+ALU = mybir.AluOpType
+
+P = 128
+PACK = 4
+PAGE = P * PACK
+T = 4096
+N = 1024
+D = 512
+DV = 128
+NQ = 128
+PAGES = N // PAGE
+POOL_PAGES = T // PAGE
+ROW = P - 1
+LIST_COLS = PAGE // 16
+
+FLOPS = 2 * NQ * N * (D + DV)
+BYTES = P * T * 4 + 16 * T + POOL_PAGES * (P * DV * 4 + 16 * DV) + P * NQ * 4 + 16 * NQ + 2 * T * 4 + 2 * NQ * DV * 4 + P * (N + PAGES * DV) // 8
+
+
+def zero_single_port(nc, ap):
+    n = ap.shape[1]
+    nc.vector.memset(ap[:, 0 : n - 1], 0)
+    nc.vector.memset(ap[:, n - 1 : n], 0)
+
+
+def tile_attend_pkv8q_rel2_kb_gate_kernel(tc, q_words, q_scales, k_words, k_scales, v_words, v_scales, vs, kb, og, offs, voffs, out):
+    nc = tc.nc
+    with ExitStack() as ctx:
+        keep = ctx.enter_context(tc.tile_pool(name="keep", bufs=1))
+        psum = ctx.enter_context(tc.psum_pool(name="psum", bufs=1))
+
+        offs_sb = keep.tile([P, N // 16], U16, name="offs_sb")
+        voffs_sb = keep.tile([P, PAGES * DV // 16], U16, name="voffs_sb")
+        kw_pool = keep.tile([P, T], I32, name="kw_pool", tag="kw_then_vs")
+        ks_pool = keep.tile([P, T], U8, name="ks_pool")
+        vw_pool = keep.tile([P, POOL_PAGES * DV], I32, name="vw_pool", tag="vw_then_vsc", align_bytes=64)
+        vsc_pool = keep.tile([P, POOL_PAGES * DV], U8, name="vsc_pool", tag="w0", align_bytes=64)
+        kb_pool = keep.tile([P, T], F32, name="kb_pool")
+        vs_pool = keep.tile([P, T], F32, name="vs_pool", tag="vs_then_vw", align_bytes=64)
+        qw = keep.tile([P, NQ], I32, name="qw", align_bytes=64)
+        qs = keep.tile([P, NQ], U8, name="qs", align_bytes=64)
+        og_sb = keep.tile([NQ, DV], F32, name="og_sb")
+        ident = keep.tile([P, P], F32, name="ident")
+
+        ks_words = ks_pool[:].bitcast(I32)
+        half = T // 8
+        nc.gpsimd.memset(qs[:].bitcast(I32), 0)
+        nc.gpsimd.memset(ks_words[:, half:], 0)
+        zero_single_port(nc, ks_words[:, :half])
+        nc.gpsimd.memset(kb_pool[0:ROW, T // 2 :], 0.0)
+        zero_single_port(nc, kb_pool[0:ROW, : T // 2])
+        make_identity(nc, ident[:])
+        nc.gpsimd.memset(vsc_pool[:].bitcast(I32), 0)
+        nc.gpsimd.memset(vs_pool[0:ROW, :], 0.0)
+
+        nc.sync.dma_start(offs_sb[:], offs)
+        nc.sync.dma_start(kb_pool[ROW:P, :], kb[0:1, :])
+        nc.sync.dma_start(vs_pool[ROW:P, :], vs[0:1, :])
+        nc.sync.dma_start(og_sb[:], og[0])
+        nc.sync.dma_start(kw_pool[:], k_words[0].rearrange("p t r -> p (t r)").bitcast(I32))
+        for g in range(4):
+            nc.scalar.dma_start(ks_words[32 * g : 32 * g + 4, :], k_scales[0, 4 * g : 4 * g + 4, :].bitcast(I32))
+        nc.scalar.dma_start(qw[:], q_words[0, 0].rearrange("p q r -> p (q r)").bitcast(I32))
+        for g in range(4):
+            nc.scalar.dma_start(qs[32 * g : 32 * g + 4, :].bitcast(I32), q_scales[0, 0, 4 * g : 4 * g + 4, :].bitcast(I32))
+        nc.sync.dma_start(voffs_sb[:], voffs)
+        nc.sync.dma_start(
+            vw_pool[:].rearrange("p (u e) -> p u e", u=POOL_PAGES),
+            v_words.rearrange("u p e r -> p u (e r)").bitcast(I32),
+        )
+        for g in range(4):
+            nc.sync.dma_start(
+                vsc_pool[32 * g : 32 * g + 4, :].bitcast(I32).rearrange("f (u e) -> f u e", u=POOL_PAGES),
+                v_scales[:, 4 * g : 4 * g + 4, :].rearrange("u f e -> f u e").bitcast(I32),
+            )
+
+        gate = keep.tile([NQ, DV], F32, name="gate")
+        nc.scalar.activation(gate[:], og_sb[:], ACT.Sigmoid)
+
+        def page_list(e):
+            return offs_sb[:, e * LIST_COLS : (e + 1) * LIST_COLS]
+
+        def turn_row(row, name, bank):
+            cols = psum.tile([P, PACK, P], F32, name=name, tag=bank)
+            for t in range(PACK):
+                nc.tensor.transpose(cols[:, t, :], row[:, t : PAGE : PACK], ident[:])
+            return cols
+
+        kb_cols = []
+        for e in range(PAGES):
+            kb_g = keep.tile([P, PAGE], F32, name=f"kb_g{e}")
+            nc.vector.tensor_copy(kb_g[:], kb_pool[:].indirect(page_list(e)))
+            turned = turn_row(kb_g[:], f"kb_turned{e}", f"kb{e}")
+            kb_col = keep.tile([P, PACK], F32, name=f"kb_col{e}")
+            nc.scalar.copy(kb_col[:], turned[:, :, ROW])
+            kb_cols.append(kb_col)
+
+        ks_g = keep.tile([P, N], U8, name="ks_g", align_bytes=64)
+        nc.vector.tensor_copy(ks_g[:], ks_pool[:].indirect(offs_sb[:]))
+
+        l_parts = psum.tile([NQ, P], F32, name="l_parts")
+        ps = []
+        for e in range(PAGES):
+            kw_g = keep.tile([P, PAGE], U32, name=f"kw_g{e}", align_bytes=64)
+            nc.vector.tensor_copy(kw_g[:], kw_pool[:].bitcast(U32).indirect(page_list(e)))
+            a_ps = psum.tile([NQ, PAGE], F32, name=f"a_ps{e}", tag=f"a{e}")
+            nc.tensor.matmul_mx(
+                a_ps[:], lhsT=qw[:].bitcast(FP8X4), lhsT_scale=qs[:],
+                rhs=kw_g[:].bitcast(FP8X4), rhs_scale=ks_g[:, e * PAGE : (e + 1) * PAGE],
+                start=True, stop=True,
+            )
+            a_sb = keep.tile([NQ, PACK, P], F32, name=f"a_sb{e}")
+            nc.scalar.copy(a_sb[:], a_ps[:].rearrange("q (s t) -> q t s", t=PACK))
+            at_ps = psum.tile([P, PACK, NQ], F32, name=f"at_ps{e}", tag=f"at{e}")
+            for t in range(PACK):
+                nc.tensor.transpose(at_ps[:, t, :], a_sb[:, t, :], ident[:])
+            r = keep.tile([P, PACK, NQ], F32, name=f"r{e}")
+            for t in range(PACK):
+                nc.scalar.activation(r[:, t, :], at_ps[:, t, :], ACT.Relu, bias=kb_cols[e][:, t : t + 1])
+            p = keep.tile([P, PACK, NQ], F32, name=f"p{e}")
+            nc.scalar.activation(p[:], r[:], ACT.Square)
+            for t in range(PACK):
+                nc.tensor.matmul(
+                    l_parts[:], lhsT=p[:, t, :], rhs=ident[:], is_transpose=True,
+                    start=(e == 0 and t == 0), stop=(e == PAGES - 1 and t == PACK - 1),
+                )
+            ps.append(p)
+
+        vs_cols = []
+        vs_g = keep.tile([P, N], F32, name="vs_g", tag="kw_then_vs")
+        for e in range(PAGES):
+            vs_page = vs_g[:, e * PAGE : (e + 1) * PAGE]
+            nc.vector.tensor_copy(vs_page, vs_pool[:].indirect(page_list(e)))
+            vs_cols.append(turn_row(vs_page, f"vs_turned{e}", ("a1", "at1")[e]))
+
+        vw_g = keep.tile([P, PAGES * DV], U32, name="vw_g", tag="vs_then_vw", align_bytes=64)
+        nc.vector.tensor_copy(vw_g[:], vw_pool[:].bitcast(U32).indirect(voffs_sb[:]))
+        vsc_g = keep.tile([P, PAGES * DV], U8, name="vsc_g", tag="vw_then_vsc", align_bytes=64)
+        nc.vector.tensor_copy(vsc_g[:], vsc_pool[:].indirect(voffs_sb[:]))
+
+        y_ps = psum.tile([NQ, DV], F32, name="y_ps")
+        for e in range(PAGES):
+            w = keep.tile([P, NQ, PACK], BF16, name=f"w{e}", tag=f"w{e}", align_bytes=64)
+            nc.vector.tensor_tensor(
+                w[:], ps[e][:].rearrange("s t q -> s q t"),
+                vs_cols[e][:, :, ROW:P].rearrange("s t o -> s o t").to_broadcast([P, NQ, PACK]), ALU.mult,
+            )
+            w_codes = keep.tile([P, NQ], U32, name=f"w_codes{e}", align_bytes=64)
+            w_scales = keep.tile([P, NQ], U8, name=f"w_scales{e}", align_bytes=64)
+            nc.vector.quantize_mx(w_codes[:].bitcast(FP8X4), w_scales[:], w[:].rearrange("s q t -> s (q t)"))
+            nc.tensor.matmul_mx(
+                y_ps[:], lhsT=w_codes[:].bitcast(FP8X4), lhsT_scale=w_scales[:],
+                rhs=vw_g[:, e * DV : (e + 1) * DV].bitcast(FP8X4), rhs_scale=vsc_g[:, e * DV : (e + 1) * DV],
+                start=(e == 0), stop=(e == PAGES - 1),
+            )
+
+        l_terms = keep.tile([NQ, P], F32, name="l_terms")
+        l_sum = keep.tile([NQ, 1], F32, name="l_sum")
+        nc.scalar.activation(l_terms[:], l_parts[:], ACT.Identity, bias=1.0 / P, accum_out=l_sum[:])
+        l_inv = keep.tile([NQ, 1], F32, name="l_inv")
+        nc.vector.reciprocal(l_inv[:], l_sum[:])
+        res = keep.tile([NQ, DV], F32, name="res")
+        nc.vector.scalar_tensor_tensor(res[:], y_ps[:], l_inv[:], gate[:], ALU.mult, ALU.mult)
+        nc.sync.dma_start(out[0], res[:])

@@ -25,6 +25,7 @@ PAGES = N // PAGE
 POOL_PAGES = T // PAGE
 ROW = P - 1
 LIST_COLS = PAGE // 16
+KW_HEAD = 1024
 
 FLOPS = 2 * NQ * N * (D + DV)
 BYTES = P * T * 4 + 16 * T + POOL_PAGES * (P * DV * 4 + 16 * DV) + P * NQ * 4 + 16 * NQ + 2 * T * 4 + 2 * NQ * DV * 4 + P * (N + PAGES * DV) // 8
@@ -46,8 +47,8 @@ def tile_attend_pkv8q_rel2_kb_gate_kernel(tc, q_words, q_scales, k_words, k_scal
         voffs_sb = keep.tile([P, PAGES * DV // 16], U16, name="voffs_sb")
         kw_pool = keep.tile([P, T], I32, name="kw_pool", tag="kw_then_vs")
         ks_pool = keep.tile([P, T], U8, name="ks_pool")
-        vw_pool = keep.tile([P, POOL_PAGES * DV], I32, name="vw_pool", tag="vw_then_vsc", align_bytes=64)
-        vsc_pool = keep.tile([P, POOL_PAGES * DV], U8, name="vsc_pool", tag="w0", align_bytes=64)
+        vw_pool = keep.tile([P, POOL_PAGES * DV], I32, name="vw_pool", tag="w0", align_bytes=64)
+        vsc_pool = keep.tile([P, POOL_PAGES * DV], U8, name="vsc_pool", tag="w_codes0", align_bytes=64)
         kb_pool = keep.tile([P, T], F32, name="kb_pool")
         vs_pool = keep.tile([P, T], F32, name="vs_pool", tag="vs_then_vw", align_bytes=64)
         qw = keep.tile([P, NQ], I32, name="qw", align_bytes=64)
@@ -66,16 +67,18 @@ def tile_attend_pkv8q_rel2_kb_gate_kernel(tc, q_words, q_scales, k_words, k_scal
         nc.gpsimd.memset(vsc_pool[:].bitcast(I32), 0)
         nc.gpsimd.memset(vs_pool[0:ROW, :], 0.0)
 
+        kw_src = k_words[0].rearrange("p t r -> p (t r)").bitcast(I32)
         nc.sync.dma_start(offs_sb[:], offs)
-        nc.sync.dma_start(kb_pool[ROW:P, :], kb[0:1, :])
-        nc.sync.dma_start(vs_pool[ROW:P, :], vs[0:1, :])
-        nc.sync.dma_start(og_sb[:], og[0])
-        nc.sync.dma_start(kw_pool[:], k_words[0].rearrange("p t r -> p (t r)").bitcast(I32))
+        nc.scalar.dma_start(kb_pool[ROW:P, :], kb[0:1, :])
+        nc.scalar.dma_start(og_sb[:], og[0])
+        nc.scalar.dma_start(vs_pool[ROW:P, :], vs[0:1, :])
+        nc.sync.dma_start(kw_pool[:, :KW_HEAD], kw_src[:, :KW_HEAD])
         for g in range(4):
-            nc.scalar.dma_start(ks_words[32 * g : 32 * g + 4, :], k_scales[0, 4 * g : 4 * g + 4, :].bitcast(I32))
-        nc.scalar.dma_start(qw[:], q_words[0, 0].rearrange("p q r -> p (q r)").bitcast(I32))
+            nc.sync.dma_start(ks_words[32 * g : 32 * g + 4, :], k_scales[0, 4 * g : 4 * g + 4, :].bitcast(I32))
+        nc.sync.dma_start(kw_pool[:, KW_HEAD:], kw_src[:, KW_HEAD:])
+        nc.sync.dma_start(qw[:], q_words[0, 0].rearrange("p q r -> p (q r)").bitcast(I32))
         for g in range(4):
-            nc.scalar.dma_start(qs[32 * g : 32 * g + 4, :].bitcast(I32), q_scales[0, 0, 4 * g : 4 * g + 4, :].bitcast(I32))
+            nc.sync.dma_start(qs[32 * g : 32 * g + 4, :].bitcast(I32), q_scales[0, 0, 4 * g : 4 * g + 4, :].bitcast(I32))
         nc.sync.dma_start(voffs_sb[:], voffs)
         nc.sync.dma_start(
             vw_pool[:].rearrange("p (u e) -> p u e", u=POOL_PAGES),
@@ -130,7 +133,7 @@ def tile_attend_pkv8q_rel2_kb_gate_kernel(tc, q_words, q_scales, k_words, k_scal
             r = keep.tile([P, PACK, NQ], F32, name=f"r{e}")
             for t in range(PACK):
                 nc.scalar.activation(r[:, t, :], at_ps[:, t, :], ACT.Relu, bias=kb_cols[e][:, t : t + 1])
-            p = keep.tile([P, PACK, NQ], F32, name=f"p{e}")
+            p = keep.tile([P, PACK, NQ], F32, name=f"p{e}", tag=f"p{e}", align_bytes=64)
             nc.scalar.activation(p[:], r[:], ACT.Square)
             for t in range(PACK):
                 nc.tensor.matmul(
@@ -148,8 +151,6 @@ def tile_attend_pkv8q_rel2_kb_gate_kernel(tc, q_words, q_scales, k_words, k_scal
 
         vw_g = keep.tile([P, PAGES * DV], U32, name="vw_g", tag="vs_then_vw", align_bytes=64)
         nc.vector.tensor_copy(vw_g[:], vw_pool[:].bitcast(U32).indirect(voffs_sb[:]))
-        vsc_g = keep.tile([P, PAGES * DV], U8, name="vsc_g", tag="vw_then_vsc", align_bytes=64)
-        nc.vector.tensor_copy(vsc_g[:], vsc_pool[:].indirect(voffs_sb[:]))
 
         y_ps = psum.tile([NQ, DV], F32, name="y_ps")
         for e in range(PAGES):
@@ -158,7 +159,10 @@ def tile_attend_pkv8q_rel2_kb_gate_kernel(tc, q_words, q_scales, k_words, k_scal
                 w[:], ps[e][:].rearrange("s t q -> s q t"),
                 vs_cols[e][:, :, ROW:P].rearrange("s t o -> s o t").to_broadcast([P, NQ, PACK]), ALU.mult,
             )
-            w_codes = keep.tile([P, NQ], U32, name=f"w_codes{e}", align_bytes=64)
+            if e == 0:
+                vsc_g = keep.tile([P, PAGES * DV], U8, name="vsc_g", tag="p0", align_bytes=64)
+                nc.vector.tensor_copy(vsc_g[:], vsc_pool[:].indirect(voffs_sb[:]))
+            w_codes = keep.tile([P, NQ], U32, name=f"w_codes{e}", tag=f"w_codes{e}", align_bytes=64)
             w_scales = keep.tile([P, NQ], U8, name=f"w_scales{e}", align_bytes=64)
             nc.vector.quantize_mx(w_codes[:].bitcast(FP8X4), w_scales[:], w[:].rearrange("s q t -> s (q t)"))
             nc.tensor.matmul_mx(

@@ -31,12 +31,6 @@ FLOPS = 2 * NQ * N * (D + DV)
 BYTES = P * T * 4 + 16 * T + POOL_PAGES * (P * DV * 4 + 16 * DV) + P * NQ * 4 + 16 * NQ + 2 * T * 4 + 2 * NQ * DV * 4 + P * (N + PAGES * DV) // 8
 
 
-def zero_single_port(nc, ap):
-    n = ap.shape[1]
-    nc.vector.memset(ap[:, 0 : n - 1], 0)
-    nc.vector.memset(ap[:, n - 1 : n], 0)
-
-
 def tile_attend_pkv8q_rel2_kb_gate_kernel(tc, q_words, q_scales, k_words, k_scales, v_words, v_scales, vs, kb, og, offs, voffs, out):
     nc = tc.nc
     with ExitStack() as ctx:
@@ -57,20 +51,18 @@ def tile_attend_pkv8q_rel2_kb_gate_kernel(tc, q_words, q_scales, k_words, k_scal
         ident = keep.tile([P, P], F32, name="ident")
 
         ks_words = ks_pool[:].bitcast(I32)
-        half = T // 8
+        nc.vector.memset(ks_words, 0)
+        nc.vector.memset(kb_pool[0:ROW, :], 0.0)
         nc.gpsimd.memset(qs[:].bitcast(I32), 0)
-        nc.gpsimd.memset(ks_words[:, half:], 0)
-        zero_single_port(nc, ks_words[:, :half])
-        nc.gpsimd.memset(kb_pool[0:ROW, T // 2 :], 0.0)
-        zero_single_port(nc, kb_pool[0:ROW, : T // 2])
-        make_identity(nc, ident[:])
         nc.gpsimd.memset(vsc_pool[:].bitcast(I32), 0)
-        nc.gpsimd.memset(vs_pool[0:ROW, :], 0.0)
+        make_identity(nc, ident[:])
+        vs_head = keep.tile([P, 8], F32, name="vs_head")
 
         kw_src = k_words[0].rearrange("p t r -> p (t r)").bitcast(I32)
         nc.sync.dma_start(offs_sb[:], offs)
         nc.scalar.dma_start(kb_pool[ROW:P, :], kb[0:1, :])
         nc.scalar.dma_start(og_sb[:], og[0])
+        nc.scalar.dma_start(vs_head[:], vs[:, 0:8])
         nc.scalar.dma_start(vs_pool[ROW:P, :], vs[0:1, :])
         nc.sync.dma_start(kw_pool[:, :KW_HEAD], kw_src[:, :KW_HEAD])
         for g in range(4):
@@ -92,6 +84,8 @@ def tile_attend_pkv8q_rel2_kb_gate_kernel(tc, q_words, q_scales, k_words, k_scal
 
         gate = keep.tile([NQ, DV], F32, name="gate")
         nc.scalar.activation(gate[:], og_sb[:], ACT.Sigmoid)
+
+        nc.scalar.copy(vs_pool[0:ROW, :], vs_head[0:ROW, 0:1].to_broadcast([ROW, T]))
 
         def page_list(e):
             return offs_sb[:, e * LIST_COLS : (e + 1) * LIST_COLS]
@@ -133,11 +127,11 @@ def tile_attend_pkv8q_rel2_kb_gate_kernel(tc, q_words, q_scales, k_words, k_scal
             r = keep.tile([P, PACK, NQ], F32, name=f"r{e}")
             for t in range(PACK):
                 nc.scalar.activation(r[:, t, :], at_ps[:, t, :], ACT.Relu, bias=kb_cols[e][:, t : t + 1])
-            p = keep.tile([P, PACK, NQ], F32, name=f"p{e}", tag=f"p{e}", align_bytes=64)
-            nc.scalar.activation(p[:], r[:], ACT.Square)
+            p = keep.tile([P, NQ, PACK], F32, name=f"p{e}", tag=f"p{e}", align_bytes=64)
+            nc.scalar.activation(p[:], r[:].rearrange("s t q -> s q t"), ACT.Square)
             for t in range(PACK):
                 nc.tensor.matmul(
-                    l_parts[:], lhsT=p[:, t, :], rhs=ident[:], is_transpose=True,
+                    l_parts[:], lhsT=p[:, :, t], rhs=ident[:], is_transpose=True,
                     start=(e == 0 and t == 0), stop=(e == PAGES - 1 and t == PACK - 1),
                 )
             ps.append(p)
@@ -156,7 +150,7 @@ def tile_attend_pkv8q_rel2_kb_gate_kernel(tc, q_words, q_scales, k_words, k_scal
         for e in range(PAGES):
             w = keep.tile([P, NQ, PACK], BF16, name=f"w{e}", tag=f"w{e}", align_bytes=64)
             nc.vector.tensor_tensor(
-                w[:], ps[e][:].rearrange("s t q -> s q t"),
+                w[:], ps[e][:],
                 vs_cols[e][:, :, ROW:P].rearrange("s t o -> s o t").to_broadcast([P, NQ, PACK]), ALU.mult,
             )
             if e == 0:

from contextlib import ExitStack

import concourse.mybir as mybir
from concourse.masks import make_identity

F32 = mybir.dt.float32
BF16 = mybir.dt.bfloat16
I32 = mybir.dt.int32
U32 = mybir.dt.uint32
U16 = mybir.dt.uint16
U8 = mybir.dt.uint8
FP8X4 = mybir.dt.float8_e4m3fn_x4
ACT = mybir.ActivationFunctionType
ALU = mybir.AluOpType

P = 128
PACK = 4
PAGE = P * PACK
T = 4096
N = 1024
D = 512
DV = 128
NQ = 128
PAGES = N // PAGE
POOL_PAGES = T // PAGE
ROW = P - 1
LIST_COLS = PAGE // 16
KW_HEAD = 1024

FLOPS = 2 * NQ * N * (D + DV)
BYTES = P * T * 4 + 16 * T + POOL_PAGES * (P * DV * 4 + 16 * DV) + P * NQ * 4 + 16 * NQ + 2 * T * 4 + 2 * NQ * DV * 4 + P * (N + PAGES * DV) // 8


def tile_attend_pkv8q_rel2_kb_gate_kernel(tc, q_words, q_scales, k_words, k_scales, v_words, v_scales, vs, kb, og, offs, voffs, out):
    nc = tc.nc
    with ExitStack() as ctx:
        keep = ctx.enter_context(tc.tile_pool(name="keep", bufs=1))
        psum = ctx.enter_context(tc.psum_pool(name="psum", bufs=1))

        offs_sb = keep.tile([P, N // 16], U16, name="offs_sb")
        voffs_sb = keep.tile([P, PAGES * DV // 16], U16, name="voffs_sb")
        kw_pool = keep.tile([P, T], I32, name="kw_pool", tag="kw_then_vs")
        ks_pool = keep.tile([P, T], U8, name="ks_pool")
        vw_pool = keep.tile([P, POOL_PAGES * DV], I32, name="vw_pool", tag="w0", align_bytes=64)
        vsc_pool = keep.tile([P, POOL_PAGES * DV], U8, name="vsc_pool", tag="w_codes0", align_bytes=64)
        kb_pool = keep.tile([P, T], F32, name="kb_pool")
        vs_pool = keep.tile([P, T], F32, name="vs_pool", tag="vs_then_vw", align_bytes=64)
        qw = keep.tile([P, NQ], I32, name="qw", align_bytes=64)
        qs = keep.tile([P, NQ], U8, name="qs", align_bytes=64)
        og_sb = keep.tile([NQ, DV], F32, name="og_sb")
        ident = keep.tile([P, P], F32, name="ident")

        ks_words = ks_pool[:].bitcast(I32)
        nc.vector.memset(ks_words, 0)
        nc.vector.memset(kb_pool[0:ROW, :], 0.0)
        nc.gpsimd.memset(qs[:].bitcast(I32), 0)
        nc.gpsimd.memset(vsc_pool[:].bitcast(I32), 0)
        make_identity(nc, ident[:])
        vs_head = keep.tile([P, 8], F32, name="vs_head")

        kw_src = k_words[0].rearrange("p t r -> p (t r)").bitcast(I32)
        nc.sync.dma_start(offs_sb[:], offs)
        nc.scalar.dma_start(kb_pool[ROW:P, :], kb[0:1, :])
        nc.scalar.dma_start(og_sb[:], og[0])
        nc.scalar.dma_start(vs_head[:], vs[:, 0:8])
        nc.scalar.dma_start(vs_pool[ROW:P, :], vs[0:1, :])
        nc.sync.dma_start(kw_pool[:, :KW_HEAD], kw_src[:, :KW_HEAD])
        for g in range(4):
            nc.sync.dma_start(ks_words[32 * g : 32 * g + 4, :], k_scales[0, 4 * g : 4 * g + 4, :].bitcast(I32))
        nc.sync.dma_start(kw_pool[:, KW_HEAD:], kw_src[:, KW_HEAD:])
        nc.sync.dma_start(qw[:], q_words[0, 0].rearrange("p q r -> p (q r)").bitcast(I32))
        for g in range(4):
            nc.sync.dma_start(qs[32 * g : 32 * g + 4, :].bitcast(I32), q_scales[0, 0, 4 * g : 4 * g + 4, :].bitcast(I32))
        nc.sync.dma_start(voffs_sb[:], voffs)
        nc.sync.dma_start(
            vw_pool[:].rearrange("p (u e) -> p u e", u=POOL_PAGES),
            v_words.rearrange("u p e r -> p u (e r)").bitcast(I32),
        )
        for g in range(4):
            nc.sync.dma_start(
                vsc_pool[32 * g : 32 * g + 4, :].bitcast(I32).rearrange("f (u e) -> f u e", u=POOL_PAGES),
                v_scales[:, 4 * g : 4 * g + 4, :].rearrange("u f e -> f u e").bitcast(I32),
            )

        gate = keep.tile([NQ, DV], F32, name="gate")
        nc.scalar.activation(gate[:], og_sb[:], ACT.Sigmoid)

        nc.scalar.copy(vs_pool[0:ROW, :], vs_head[0:ROW, 0:1].to_broadcast([ROW, T]))

        def page_list(e):
            return offs_sb[:, e * LIST_COLS : (e + 1) * LIST_COLS]

        def turn_row(row, name, bank):
            cols = psum.tile([P, PACK, P], F32, name=name, tag=bank)
            for t in range(PACK):
                nc.tensor.transpose(cols[:, t, :], row[:, t : PAGE : PACK], ident[:])
            return cols

        kb_cols = []
        for e in range(PAGES):
            kb_g = keep.tile([P, PAGE], F32, name=f"kb_g{e}")
            nc.vector.tensor_copy(kb_g[:], kb_pool[:].indirect(page_list(e)))
            turned = turn_row(kb_g[:], f"kb_turned{e}", f"kb{e}")
            kb_col = keep.tile([P, PACK], F32, name=f"kb_col{e}")
            nc.scalar.copy(kb_col[:], turned[:, :, ROW])
            kb_cols.append(kb_col)

        ks_g = keep.tile([P, N], U8, name="ks_g", align_bytes=64)
        nc.vector.tensor_copy(ks_g[:], ks_pool[:].indirect(offs_sb[:]))

        l_parts = psum.tile([NQ, P], F32, name="l_parts")
        ps = []
        for e in range(PAGES):
            kw_g = keep.tile([P, PAGE], U32, name=f"kw_g{e}", align_bytes=64)
            nc.vector.tensor_copy(kw_g[:], kw_pool[:].bitcast(U32).indirect(page_list(e)))
            a_ps = psum.tile([NQ, PAGE], F32, name=f"a_ps{e}", tag=f"a{e}")
            nc.tensor.matmul_mx(
                a_ps[:], lhsT=qw[:].bitcast(FP8X4), lhsT_scale=qs[:],
                rhs=kw_g[:].bitcast(FP8X4), rhs_scale=ks_g[:, e * PAGE : (e + 1) * PAGE],
                start=True, stop=True,
            )
            a_sb = keep.tile([NQ, PACK, P], F32, name=f"a_sb{e}")
            nc.scalar.copy(a_sb[:], a_ps[:].rearrange("q (s t) -> q t s", t=PACK))
            at_ps = psum.tile([P, PACK, NQ], F32, name=f"at_ps{e}", tag=f"at{e}")
            for t in range(PACK):
                nc.tensor.transpose(at_ps[:, t, :], a_sb[:, t, :], ident[:])
            r = keep.tile([P, PACK, NQ], F32, name=f"r{e}")
            for t in range(PACK):
                nc.scalar.activation(r[:, t, :], at_ps[:, t, :], ACT.Relu, bias=kb_cols[e][:, t : t + 1])
            p = keep.tile([P, NQ, PACK], F32, name=f"p{e}", tag=f"p{e}", align_bytes=64)
            nc.scalar.activation(p[:], r[:].rearrange("s t q -> s q t"), ACT.Square)
            for t in range(PACK):
                nc.tensor.matmul(
                    l_parts[:], lhsT=p[:, :, t], rhs=ident[:], is_transpose=True,
                    start=(e == 0 and t == 0), stop=(e == PAGES - 1 and t == PACK - 1),
                )
            ps.append(p)

        vs_cols = []
        vs_g = keep.tile([P, N], F32, name="vs_g", tag="kw_then_vs")
        for e in range(PAGES):
            vs_page = vs_g[:, e * PAGE : (e + 1) * PAGE]
            nc.vector.tensor_copy(vs_page, vs_pool[:].indirect(page_list(e)))
            vs_cols.append(turn_row(vs_page, f"vs_turned{e}", ("a1", "at1")[e]))

        vw_g = keep.tile([P, PAGES * DV], U32, name="vw_g", tag="vs_then_vw", align_bytes=64)
        nc.vector.tensor_copy(vw_g[:], vw_pool[:].bitcast(U32).indirect(voffs_sb[:]))

        y_ps = psum.tile([NQ, DV], F32, name="y_ps")
        for e in range(PAGES):
            w = keep.tile([P, NQ, PACK], BF16, name=f"w{e}", tag=f"w{e}", align_bytes=64)
            nc.vector.tensor_tensor(
                w[:], ps[e][:],
                vs_cols[e][:, :, ROW:P].rearrange("s t o -> s o t").to_broadcast([P, NQ, PACK]), ALU.mult,
            )
            if e == 0:
                vsc_g = keep.tile([P, PAGES * DV], U8, name="vsc_g", tag="p0", align_bytes=64)
                nc.vector.tensor_copy(vsc_g[:], vsc_pool[:].indirect(voffs_sb[:]))
            w_codes = keep.tile([P, NQ], U32, name=f"w_codes{e}", tag=f"w_codes{e}", align_bytes=64)
            w_scales = keep.tile([P, NQ], U8, name=f"w_scales{e}", align_bytes=64)
            nc.vector.quantize_mx(w_codes[:].bitcast(FP8X4), w_scales[:], w[:].rearrange("s q t -> s (q t)"))
            nc.tensor.matmul_mx(
                y_ps[:], lhsT=w_codes[:].bitcast(FP8X4), lhsT_scale=w_scales[:],
                rhs=vw_g[:, e * DV : (e + 1) * DV].bitcast(FP8X4), rhs_scale=vsc_g[:, e * DV : (e + 1) * DV],
                start=(e == 0), stop=(e == PAGES - 1),
            )

        l_terms = keep.tile([NQ, P], F32, name="l_terms")
        l_sum = keep.tile([NQ, 1], F32, name="l_sum")
        nc.scalar.activation(l_terms[:], l_parts[:], ACT.Identity, bias=1.0 / P, accum_out=l_sum[:])
        l_inv = keep.tile([NQ, 1], F32, name="l_inv")
        nc.vector.reciprocal(l_inv[:], l_sum[:])
        res = keep.tile([NQ, DV], F32, name="res")
        nc.vector.scalar_tensor_tensor(res[:], y_ps[:], l_inv[:], gate[:], ALU.mult, ALU.mult)
        nc.sync.dma_start(out[0], res[:])
